import numpy as np
import ml_dtypes


def mxq(x, axis, fmt="e4m3"):
    dtype, down = {"e4m3": (ml_dtypes.float8_e4m3fn, 7), "e5m2": (ml_dtypes.float8_e5m2, 14)}[fmt]
    v = np.moveaxis(np.asarray(x, np.float32).astype(ml_dtypes.bfloat16).astype(np.float64), axis, -1)
    blocks = v.reshape(v.shape[:-1] + (-1, 32))
    amax = np.abs(blocks).max(-1, keepdims=True)
    byte = np.maximum(np.where(amax > 0, np.frexp(amax)[1] - 1 + 127, 0) - down, 1)
    scale = np.exp2(byte - 127.0)
    codes = (blocks / scale).astype(np.float32).astype(dtype).astype(np.float64)
    return np.moveaxis((codes * scale).reshape(v.shape), -1, axis)


WIDE = False


def mx_kscale(k):
    if not WIDE:
        return np.ones(k)
    levels = np.array([10, -10, 5, -5, 0])
    if k % 512:
        return np.exp2(np.random.permutation(np.resize(levels, k // 32))).repeat(32)
    a = np.empty((k // 512, 16))
    for p in range(k // 512):
        a[p, :8] = np.random.permutation(np.resize(levels, 8))
        for g in range(8):
            far = levels[np.abs(levels - a[p, g]) >= 10]
            a[p, g + 8] = far[np.random.randint(len(far))]
    return np.exp2(a.ravel()).repeat(32)


def f64(x):
    return np.asarray(x).astype(np.float64)


def striped(idx):
    return np.tile(idx.reshape(-1, 16).T, (8, 1)).astype(np.uint16)


def unstriped(offs):
    return offs[:16].T.reshape(-1).astype(np.int64)


def pack_weight(w):
    k, n = w.shape
    w = f64(np.asarray(w, np.float32).astype(ml_dtypes.bfloat16)).reshape(k // 32, 32, n)
    amax = np.abs(w).max(1)
    byte = np.clip(np.where(amax > 0, np.frexp(amax)[1] - 1 + 127 - 7, 1), 1, 254)
    scaled = (w * np.exp2(127.0 - byte)[:, None, :]).reshape(k, n).astype(np.float32)
    words = np.ascontiguousarray(scaled.reshape(k // 512, 128, 4, n).transpose(0, 1, 3, 2)).astype(ml_dtypes.float8_e4m3fn).view(np.uint8)
    return words, np.ascontiguousarray(byte.astype(np.uint8).reshape(k // 512, 16, n))


def unpack_weight(words, scales):
    g, p, n, _ = words.shape
    vals = np.ascontiguousarray(words).view(ml_dtypes.float8_e4m3fn).astype(np.float64) * np.repeat(np.exp2(scales.astype(np.float64) - 127.0), 8, axis=1)[..., None]
    return vals.transpose(0, 1, 3, 2).reshape(g * 512, n)


K, T, S, N, H = 512, 1024, 512, 128, 512


def setup_inputs():
    n = np.random.standard_normal
    s = mx_kscale(K)[:, None]
    u = mx_kscale(H)
    packed_xT = pack_weight(n((K, T)) * s)
    return {
        "x_words": packed_xT[0],
        "x_scales": packed_xT[1],
        "w1": (n((K, H)) / np.sqrt(K) / s).astype(np.float32),
        "h1": (np.random.uniform(0.1, 1.5, (H, S))).astype(np.float32),
        "h2": (np.random.uniform(0.1, 1.5, (H, S))).astype(np.float32),
        "rho": (np.random.uniform(0.1, 0.8, (H, S))).astype(np.float32),
        "unit": (np.random.uniform(0.6, 1.4, (H, 1)) * u[:, None]).astype(np.float32),
        "w2": (n((H, N)) / np.sqrt(H) / u[:, None]).astype(np.float32),
        "offs": striped(np.random.permutation(T)[:S]),
        "n1": striped(np.random.permutation(S)),
        "n2": striped(np.random.permutation(S)),
    }


def reference(x_words, x_scales, w1, h1, h2, rho, unit, w2, offs, n1, n2):
    c1 = np.exp(-1.0 * f64(h1))
    c2 = np.exp(-1.0 * f64(h2))
    dn = -1.0 * (0.9 * ((f64(rho)) ** 2)) + 1.05
    we1 = (c1 - (f64(rho) * c2)) / dn
    xq = unpack_weight(x_words, x_scales)[:, unstriped(offs)]
    y = mxq(f64(w1), 0, "e4m3").T @ xq
    y1 = y[:, unstriped(n1)]
    we2 = (c2 - (f64(rho) * c1)) / dn
    y2 = y[:, unstriped(n2)]
    kr = we1 * y1 + we2 * y2
    hid = f64(unit) * kr
    return mxq(f64(w2), 0, "e4m3").T @ mxq(hid, 0, "e4m3")

@@ -1,0 +1,184 @@
+from contextlib import ExitStack
+
+import concourse.mybir as mybir
+from concourse.masks import make_identity
+
+FLOPS = 335544320
+
+F32 = mybir.dt.float32
+BF16 = mybir.dt.bfloat16
+I32 = mybir.dt.int32
+U32 = mybir.dt.uint32
+U16 = mybir.dt.uint16
+U8 = mybir.dt.uint8
+FP8X4 = mybir.dt.float8_e4m3fn_x4
+ALU = mybir.AluOpType
+ACT = mybir.ActivationFunctionType
+
+P = 128
+T, S, N, H = 1024, 512, 128, 512
+NT = H // P
+PIECES = ((0, 256), (256, 128), (384, 128))
+ON_SCALAR = {(0, 0), (1, 0), (2, 0), (3, 0)}
+
+
+def tile_picked_yskrig_est_p_kernel(tc, x_words, x_scales, w1, h1, h2, rho, unit, w2, offs, n1, n2, out):
+    nc = tc.nc
+    with ExitStack() as ctx:
+        sb = ctx.enter_context(tc.tile_pool(name="sb", bufs=1))
+        rot = ctx.enter_context(tc.psum_pool(name="rot", bufs=4))
+        acc = ctx.enter_context(tc.psum_pool(name="acc", bufs=1))
+
+        offs_sb = sb.tile([P, S // 16], U16, name="offs_sb")
+        n_sb = [sb.tile([P, S // 16], U16, name="n_sb%d" % (l,)) for l in range(2)]
+        xw = sb.tile([P, T], I32, name="xw", align_bytes=64)
+        xs = sb.tile([P, T], U8, name="xs", align_bytes=64)
+        ident = sb.tile([P, P], F32, name="ident")
+        nc.vector.memset(xs[:].bitcast(I32), 0)
+        make_identity(nc, ident[:])
+
+        hs = [[sb.tile([P, S], F32, name="h%d_%d" % (l, t,)) for t in range(NT)] for l in range(2)]
+        rh = [sb.tile([P, S], F32, name="rho_%d" % (t,)) for t in range(NT)]
+        w1_raw = sb.tile([P, 4, H], F32, name="w1_raw")
+        w2_raw = sb.tile([P, 4, N], F32, name="w2_raw")
+        unit_sb = sb.tile([P, NT], F32, name="unit_sb")
+
+        def load_rows(t):
+            rows = slice(t * P, (t + 1) * P)
+            nc.sync.dma_start(hs[0][t][:], h1[rows, :])
+            nc.sync.dma_start(hs[1][t][:], h2[rows, :])
+            nc.sync.dma_start(rh[t][:], rho[rows, :])
+
+        nc.sync.dma_start(xw[:], x_words[0].rearrange("p n t -> p (n t)").bitcast(I32))
+        nc.sync.dma_start(offs_sb[:], offs)
+        for q in range(4):
+            nc.sync.dma_start(xs[32 * q : 32 * q + 4, :].bitcast(I32), x_scales[0, 4 * q : 4 * q + 4, :].bitcast(I32))
+        load_rows(0)
+        load_rows(1)
+        nc.sync.dma_start(w1_raw[:], w1.rearrange("(p j) c -> p j c", j=4))
+        load_rows(2)
+        with nc.allow_non_contiguous_dma(reason="one value a partition and row tile"):
+            nc.sync.dma_start(unit_sb[:], unit.rearrange("(t p) o -> p (t o)", p=P))
+        nc.sync.dma_start(n_sb[0][:], n1)
+        nc.sync.dma_start(n_sb[1][:], n2)
+        load_rows(3)
+        nc.sync.dma_start(w2_raw[:], w2.rearrange("(p j) c -> p j c", j=4))
+
+        gw = sb.tile([P, S], U32, name="gw", align_bytes=64)
+        gs = sb.tile([P, S], U8, name="gs", align_bytes=64)
+        nc.vector.tensor_copy(gw[:], xw[:].bitcast(U32).indirect(offs_sb[:]))
+        nc.vector.tensor_copy(gs[:], xs[:].indirect(offs_sb[:]))
+
+        cs = [[sb.tile([P, S], F32, name="c%d_%d" % (l, t,)) for t in range(NT)] for l in range(2)]
+        ms = [[sb.tile([P, S], F32, name="m%d_%d" % (l, t,)) for t in range(NT)] for l in range(2)]
+        ws = [[sb.tile([P, S], F32, name="a%d_%d" % (l, t,)) for t in range(NT)] for l in range(2)]
+        sq = sb.tile([P, 4, NT, P], F32, name="sq")
+        d2 = sb.tile([P, 4, NT, P], F32, name="d2")
+
+        def weights(t):
+            for l in range(2):
+                nc.scalar.activation(cs[l][t][:], hs[l][t][:], ACT.Exp, scale=-1.0)
+            for l in range(2):
+                nc.vector.tensor_tensor(ms[l][t][:], rh[t][:], cs[1 - l][t][:], ALU.mult)
+            for l in range(2):
+                nc.vector.tensor_tensor(ws[l][t][:], cs[l][t][:], ms[l][t][:], ALU.subtract)
+            bank = rot.tile([P, 4, P], F32, name="bank")
+            for jb in range(4):
+                nc.tensor.transpose(bank[:, jb, :], rh[t][:, jb * P : (jb + 1) * P], ident[:])
+            nc.scalar.activation(sq[:, :, t, :], bank[:], ACT.Square)
+            nc.scalar.activation(d2[:, :, t, :], sq[:, :, t, :], ACT.Square, scale=-0.45, bias=0.525)
+
+        def side_by_side(dst, src):
+            return dst.rearrange("p (c i) j -> p c j i", i=4), src.rearrange("p j (c i) -> p c j i", i=4)
+
+        w1b = sb.tile([P, H, 4], BF16, name="w1b", align_bytes=64)
+        w1q = sb.tile([P, H], U32, name="w1q", align_bytes=64)
+        w1s = sb.tile([P, H], U8, name="w1s", align_bytes=64)
+        y = [sb.tile([P, S], F32, name="y%d" % (t,)) for t in range(NT)]
+
+        def first_product(t):
+            bank = rot.tile([P, S], F32, name="bank")
+            cols = slice(t * P, (t + 1) * P)
+            nc.tensor.matmul_mx(out=bank[:], lhsT=w1q[:, cols].bitcast(FP8X4), lhsT_scale=w1s[:, cols],
+                                rhs=gw[:].bitcast(FP8X4), rhs_scale=gs[:], start=True, stop=True)
+            nc.scalar.activation(y[t][:], bank[:], ACT.Copy, scale=unit_sb[:, t : t + 1])
+
+        weights(0)
+        weights(1)
+        nc.vector.tensor_copy(*side_by_side(w1b[:], w1_raw[:]))
+        nc.vector.quantize_mx(out=w1q[:].bitcast(FP8X4), scales=w1s[:], in_=w1b[:].rearrange("p c j -> p (c j)"))
+        weights(2)
+        first_product(0)
+        first_product(1)
+        weights(3)
+        first_product(2)
+        first_product(3)
+
+        w2b = sb.tile([P, N, 4], BF16, name="w2b", align_bytes=64)
+        w2q = sb.tile([P, N], U32, name="w2q", align_bytes=64)
+        w2s = sb.tile([P, N], U8, name="w2s", align_bytes=64)
+
+        inv = sb.tile([P, 4, H], F32, name="inv")
+        sgn = sb.tile([P, 4, H], BF16, name="sgn")
+        sq3 = sq[:].rearrange("p b t q -> p b (t q)")
+        d23 = d2[:].rearrange("p b t q -> p b (t q)")
+        sums = [acc.tile([P, NT, P], F32, name="sum%d" % (b,)) for b in range(4)]
+
+        def inverse(j0, n):
+            b = slice(j0 // P, (j0 + n) // P)
+            nc.scalar.activation(inv[:, b, :], d23[:, b, :], ACT.Abs_reciprocal_sqrt)
+            nc.vector.tensor_scalar(sgn[:, b, :], sq3[:, b, :], 1.05 / 0.9, 0.5, ALU.is_lt, ALU.subtract)
+
+        def products(j0, n):
+            js = slice(j0, j0 + n)
+            lc = slice(j0 // 16, (j0 + n) // 16)
+            for t in range(NT):
+                pr = []
+                for l in (1, 0):
+                    p_ = sb.tile([P, n], F32, name="p%d_%d_%d" % (j0, t, l,))
+                    wt = ws[l][t][:, js]
+                    if (t, l) in ON_SCALAR:
+                        yg = sb.tile([P, n], F32, name="yg%d_%d_%d" % (j0, t, l,))
+                        nc.scalar.activation(yg[:], y[t][:].indirect(n_sb[l][:, lc]), ACT.Copy)
+                        nc.vector.tensor_tensor(p_[:], yg[:], wt, ALU.mult)
+                    else:
+                        nc.vector.tensor_tensor(p_[:], y[t][:].indirect(n_sb[l][:, lc]), wt, ALU.mult)
+                    pr.append(p_)
+                for b in range(n // P):
+                    for l in range(2):
+                        nc.tensor.matmul(sums[j0 // P + b][:, t, :], pr[l][:, b * P : (b + 1) * P], ident[:],
+                                         is_transpose=True, start=(l == 0), stop=(l == 1))
+
+        def finish(j0, n):
+            nb = n // P
+            mag = sb.tile([P, nb, H], BF16, name="mag%d" % (j0,))
+            hid_t = sb.tile([P, nb, H], BF16, name="hid_t%d" % (j0,))
+            for b in range(nb):
+                nc.vector.tensor_tensor(mag[:, b, :], sums[j0 // P + b][:].rearrange("p t q -> p (t q)"), inv[:, j0 // P + b, :], ALU.mult)
+            nc.vector.tensor_tensor(hid_t[:], mag[:], sgn[:, j0 // P : j0 // P + nb, :], ALU.mult)
+            back = rot.tile([P, nb, 2, P], F32, name="bank")
+            for b in range(nb):
+                words = hid_t[:, b, :].bitcast(F32)
+                for u in range(2):
+                    nc.tensor.transpose(back[:, b, u, :], words[:, u : H // 2 : 2], ident[:])
+            hid = sb.tile([P, n * 4], BF16, name="hid%d" % (j0,), align_bytes=64)
+            nc.scalar.copy(hid[:].bitcast(F32).rearrange("p (b j u) -> p b j u", b=nb, u=2), back[:].rearrange("p b u j -> p b j u"))
+            hq = sb.tile([P, n], U32, name="hq%d" % (j0,), align_bytes=64)
+            hsc = sb.tile([P, n], U8, name="hsc%d" % (j0,), align_bytes=64)
+            nc.vector.quantize_mx(out=hq[:].bitcast(FP8X4), scales=hsc[:], in_=hid[:])
+            bank = rot.tile([P, n], F32, name="bank")
+            nc.tensor.matmul_mx(out=bank[:], lhsT=w2q[:].bitcast(FP8X4), lhsT_scale=w2s[:],
+                                rhs=hq[:].bitcast(FP8X4), rhs_scale=hsc[:], start=True, stop=True)
+            res = sb.tile([P, n], F32, name="res%d" % (j0,))
+            nc.scalar.copy(res[:], bank[:])
+            nc.sync.dma_start(out[:, j0 : j0 + n], res[:])
+
+        products(*PIECES[0])
+        inverse(*PIECES[0])
+        nc.scalar.copy(*side_by_side(w2b[:], w2_raw[:]))
+        nc.vector.quantize_mx(out=w2q[:].bitcast(FP8X4), scales=w2s[:], in_=w2b[:].rearrange("p c j -> p (c j)"))
+        for k in range(1, len(PIECES)):
+            products(*PIECES[k])
+            inverse(*PIECES[k])
+            finish(*PIECES[k - 1])
+        finish(*PIECES[-1])

@@ -19,7 +19,10 @@ P = 128
 T, S, N, H = 1024, 512, 128, 512
 NT = H // P
 PIECES = ((0, 256), (256, 128), (384, 128))
-ON_SCALAR = {(0, 0), (1, 0), (2, 0), (3, 0)}
+
+
+def scalar_lists(k, t0):
+    return 2 if k > 0 else 0
 
 
 def tile_picked_yskrig_est_p_kernel(tc, x_words, x_scales, w1, h1, h2, rho, unit, w2, offs, n1, n2, out):
@@ -34,10 +37,9 @@ def tile_picked_yskrig_est_p_kernel(tc, x_words, x_scales, w1, h1, h2, rho, unit
         xw = sb.tile([P, T], I32, name="xw", align_bytes=64)
         xs = sb.tile([P, T], U8, name="xs", align_bytes=64)
         ident = sb.tile([P, P], F32, name="ident")
-        nc.vector.memset(xs[:].bitcast(I32), 0)
         make_identity(nc, ident[:])
 
-        hs = [[sb.tile([P, S], F32, name="h%d_%d" % (l, t,)) for t in range(NT)] for l in range(2)]
+        hs = [sb.tile([P, 2, S], F32, name="h_%d" % (t,)) for t in range(NT)]
         rh = [sb.tile([P, S], F32, name="rho_%d" % (t,)) for t in range(NT)]
         w1_raw = sb.tile([P, 4, H], F32, name="w1_raw")
         w2_raw = sb.tile([P, 4, N], F32, name="w2_raw")
@@ -45,43 +47,55 @@ def tile_picked_yskrig_est_p_kernel(tc, x_words, x_scales, w1, h1, h2, rho, unit
 
         def load_rows(t):
             rows = slice(t * P, (t + 1) * P)
-            nc.sync.dma_start(hs[0][t][:], h1[rows, :])
-            nc.sync.dma_start(hs[1][t][:], h2[rows, :])
-            nc.sync.dma_start(rh[t][:], rho[rows, :])
+            nc.sync.dma_start(hs[t][:, 1, :], h2[rows, :])
+            if t == 0:
+                nc.sync.dma_start(rh[t][:], rho[rows, :])
+            nc.sync.dma_start(hs[t][:, 0, :], h1[rows, :])
+            if t > 0:
+                nc.sync.dma_start(rh[t][:], rho[rows, :])
 
-        nc.sync.dma_start(xw[:], x_words[0].rearrange("p n t -> p (n t)").bitcast(I32))
+        def load_x():
+            nc.sync.dma_start(xw[:], x_words[0].rearrange("p n t -> p (n t)").bitcast(I32))
+
+        def load_w1():
+            nc.sync.dma_start(w1_raw[:], w1.rearrange("(p j) c -> p j c", j=4))
+            with nc.allow_non_contiguous_dma(reason="one value a partition and row tile"):
+                nc.sync.dma_start(unit_sb[:], unit.rearrange("(t p) o -> p (t o)", p=P))
+            nc.sync.dma_start(n_sb[0][:], n1)
+            nc.sync.dma_start(n_sb[1][:], n2)
+
         nc.sync.dma_start(offs_sb[:], offs)
         for q in range(4):
-            nc.sync.dma_start(xs[32 * q : 32 * q + 4, :].bitcast(I32), x_scales[0, 4 * q : 4 * q + 4, :].bitcast(I32))
+            nc.sync.dma_start(xs[32 * q : 32 * q + 32, :].bitcast(I32), x_scales[0, 4 * q : 4 * q + 4, :].bitcast(I32).partition_broadcast(8))
         load_rows(0)
         load_rows(1)
-        nc.sync.dma_start(w1_raw[:], w1.rearrange("(p j) c -> p j c", j=4))
+        load_x()
         load_rows(2)
-        with nc.allow_non_contiguous_dma(reason="one value a partition and row tile"):
-            nc.sync.dma_start(unit_sb[:], unit.rearrange("(t p) o -> p (t o)", p=P))
-        nc.sync.dma_start(n_sb[0][:], n1)
-        nc.sync.dma_start(n_sb[1][:], n2)
         load_rows(3)
+        load_w1()
         nc.sync.dma_start(w2_raw[:], w2.rearrange("(p j) c -> p j c", j=4))
 
         gw = sb.tile([P, S], U32, name="gw", align_bytes=64)
         gs = sb.tile([P, S], U8, name="gs", align_bytes=64)
-        nc.vector.tensor_copy(gw[:], xw[:].bitcast(U32).indirect(offs_sb[:]))
         nc.vector.tensor_copy(gs[:], xs[:].indirect(offs_sb[:]))
+        nc.vector.tensor_copy(gw[:], xw[:].bitcast(U32).indirect(offs_sb[:]))
 
-        cs = [[sb.tile([P, S], F32, name="c%d_%d" % (l, t,)) for t in range(NT)] for l in range(2)]
-        ms = [[sb.tile([P, S], F32, name="m%d_%d" % (l, t,)) for t in range(NT)] for l in range(2)]
-        ws = [[sb.tile([P, S], F32, name="a%d_%d" % (l, t,)) for t in range(NT)] for l in range(2)]
+        cs = [sb.tile([P, 2, S], F32, name="c_%d" % (t,)) for t in range(NT)]
+        ms = [sb.tile([P, 2, S], F32, name="m_%d" % (t,)) for t in range(NT)]
+        ws = sb.tile([P, NT, 2, S], F32, name="ws")
         sq = sb.tile([P, 4, NT, P], F32, name="sq")
         d2 = sb.tile([P, 4, NT, P], F32, name="d2")
 
         def weights(t):
-            for l in range(2):
-                nc.scalar.activation(cs[l][t][:], hs[l][t][:], ACT.Exp, scale=-1.0)
-            for l in range(2):
-                nc.vector.tensor_tensor(ms[l][t][:], rh[t][:], cs[1 - l][t][:], ALU.mult)
-            for l in range(2):
-                nc.vector.tensor_tensor(ws[l][t][:], cs[l][t][:], ms[l][t][:], ALU.subtract)
+            if t == 0:
+                for l in (1, 0):
+                    nc.scalar.activation(cs[t][:, l, :], hs[t][:, l, :], ACT.Exp, scale=-1.0)
+                    nc.vector.tensor_tensor(ms[t][:, 1 - l, :], rh[t][:], cs[t][:, l, :], ALU.mult)
+                nc.vector.tensor_tensor(ws[:, t, :, :], cs[t][:], ms[t][:], ALU.subtract)
+            else:
+                nc.scalar.activation(cs[t][:], hs[t][:], ACT.Exp, scale=-1.0)
+                nc.vector.tensor_tensor(ms[t][:], rh[t][:].unsqueeze(1).to_broadcast([P, 2, S]), cs[t][:], ALU.mult)
+                nc.vector.tensor_tensor(ws[:, t, :, :], cs[t][:], ms[t][:, ::-1, :], ALU.subtract)
             bank = rot.tile([P, 4, P], F32, name="bank")
             for jb in range(4):
                 nc.tensor.transpose(bank[:, jb, :], rh[t][:, jb * P : (jb + 1) * P], ident[:])
@@ -105,12 +119,12 @@ def tile_picked_yskrig_est_p_kernel(tc, x_words, x_scales, w1, h1, h2, rho, unit
 
         weights(0)
         weights(1)
+        weights(2)
+        weights(3)
         nc.vector.tensor_copy(*side_by_side(w1b[:], w1_raw[:]))
         nc.vector.quantize_mx(out=w1q[:].bitcast(FP8X4), scales=w1s[:], in_=w1b[:].rearrange("p c j -> p (c j)"))
-        weights(2)
         first_product(0)
         first_product(1)
-        weights(3)
         first_product(2)
         first_product(3)
 
@@ -124,38 +138,50 @@ def tile_picked_yskrig_est_p_kernel(tc, x_words, x_scales, w1, h1, h2, rho, unit
         d23 = d2[:].rearrange("p b t q -> p b (t q)")
         sums = [acc.tile([P, NT, P], F32, name="sum%d" % (b,)) for b in range(4)]
 
-        def inverse(j0, n):
+        rcp = sb.tile([P, H], F32, name="rcp")
+
+        def inverse(k):
+            j0, n = PIECES[k]
             b = slice(j0 // P, (j0 + n) // P)
             nc.scalar.activation(inv[:, b, :], d23[:, b, :], ACT.Abs_reciprocal_sqrt)
             nc.vector.tensor_scalar(sgn[:, b, :], sq3[:, b, :], 1.05 / 0.9, 0.5, ALU.is_lt, ALU.subtract)
+            if k == len(PIECES) - 1:
+                nc.vector.tensor_tensor(rcp[:], inv[:, j0 // P, :], sgn[:, j0 // P, :], ALU.mult)
 
-        def products(j0, n):
+        def products(k):
+            j0, n = PIECES[k]
             js = slice(j0, j0 + n)
             lc = slice(j0 // 16, (j0 + n) // 16)
-            for t in range(NT):
-                pr = []
-                for l in (1, 0):
-                    p_ = sb.tile([P, n], F32, name="p%d_%d_%d" % (j0, t, l,))
-                    wt = ws[l][t][:, js]
-                    if (t, l) in ON_SCALAR:
-                        yg = sb.tile([P, n], F32, name="yg%d_%d_%d" % (j0, t, l,))
-                        nc.scalar.activation(yg[:], y[t][:].indirect(n_sb[l][:, lc]), ACT.Copy)
-                        nc.vector.tensor_tensor(p_[:], yg[:], wt, ALU.mult)
-                    else:
-                        nc.vector.tensor_tensor(p_[:], y[t][:].indirect(n_sb[l][:, lc]), wt, ALU.mult)
-                    pr.append(p_)
-                for b in range(n // P):
-                    for l in range(2):
-                        nc.tensor.matmul(sums[j0 // P + b][:, t, :], pr[l][:, b * P : (b + 1) * P], ident[:],
-                                         is_transpose=True, start=(l == 0), stop=(l == 1))
+            for t0 in (0, 2):
+                ns = scalar_lists(k, t0)
+                pr = sb.tile([P, 2, 2, n], F32, name="p%d_%d" % (k, t0,))
+                if ns:
+                    yg = sb.tile([P, 2, ns, n], F32, name="yg%d_%d" % (k, t0,))
+                    for l in range(ns):
+                        for e in range(2):
+                            nc.scalar.activation(yg[:, e, l, :], y[t0 + e][:].indirect(n_sb[l][:, lc]), ACT.Copy)
+                for e in range(2):
+                    for l in range(ns, 2):
+                        nc.vector.tensor_tensor(pr[:, e, l, :], y[t0 + e][:].indirect(n_sb[l][:, lc]), ws[:, t0 + e, l, js], ALU.mult)
+                if ns:
+                    nc.vector.tensor_tensor(pr[:, :, 0:ns, :], yg[:], ws[:, t0 : t0 + 2, 0:ns, js], ALU.mult)
+                for e in range(2):
+                    for b in range(n // P):
+                        for l in range(2):
+                            nc.tensor.matmul(sums[j0 // P + b][:, t0 + e, :], pr[:, e, l, b * P : (b + 1) * P], ident[:],
+                                             is_transpose=True, start=(l == 0), stop=(l == 1))
 
-        def finish(j0, n):
+        def finish(k):
+            j0, n = PIECES[k]
             nb = n // P
-            mag = sb.tile([P, nb, H], BF16, name="mag%d" % (j0,))
             hid_t = sb.tile([P, nb, H], BF16, name="hid_t%d" % (j0,))
-            for b in range(nb):
-                nc.vector.tensor_tensor(mag[:, b, :], sums[j0 // P + b][:].rearrange("p t q -> p (t q)"), inv[:, j0 // P + b, :], ALU.mult)
-            nc.vector.tensor_tensor(hid_t[:], mag[:], sgn[:, j0 // P : j0 // P + nb, :], ALU.mult)
+            if k == len(PIECES) - 1:
+                nc.vector.tensor_tensor(hid_t[:, 0, :], sums[j0 // P][:].rearrange("p t q -> p (t q)"), rcp[:], ALU.mult)
+            else:
+                mag = sb.tile([P, nb, H], BF16, name="mag%d" % (j0,))
+                for b in range(nb):
+                    nc.vector.tensor_tensor(mag[:, b, :], sums[j0 // P + b][:].rearrange("p t q -> p (t q)"), inv[:, j0 // P + b, :], ALU.mult)
+                nc.vector.tensor_tensor(hid_t[:], mag[:], sgn[:, j0 // P : j0 // P + nb, :], ALU.mult)
             back = rot.tile([P, nb, 2, P], F32, name="bank")
             for b in range(nb):
                 words = hid_t[:, b, :].bitcast(F32)
@@ -173,12 +199,12 @@ def tile_picked_yskrig_est_p_kernel(tc, x_words, x_scales, w1, h1, h2, rho, unit
             nc.scalar.copy(res[:], bank[:])
             nc.sync.dma_start(out[:, j0 : j0 + n], res[:])
 
-        products(*PIECES[0])
-        inverse(*PIECES[0])
+        for k in range(len(PIECES)):
+            inverse(k)
+        products(0)
         nc.scalar.copy(*side_by_side(w2b[:], w2_raw[:]))
         nc.vector.quantize_mx(out=w2q[:].bitcast(FP8X4), scales=w2s[:], in_=w2b[:].rearrange("p c j -> p (c j)"))
         for k in range(1, len(PIECES)):
-            products(*PIECES[k])
-            inverse(*PIECES[k])
-            finish(*PIECES[k - 1])
-        finish(*PIECES[-1])
+            products(k)
+            finish(k - 1)
+        finish(len(PIECES) - 1)

@@ -19,17 +19,15 @@ P = 128
 T, S, N, H = 1024, 512, 128, 512
 NT = H // P
 PIECES = ((0, 256), (256, 128), (384, 128))
-
-
-def scalar_lists(k, t0):
-    return 2 if k > 0 else 0
+LISTS_ON_SCALAR = ((0, 0, 0, 0), (1, 1, 2, 2), (2, 2, 2, 2))
+GROUPS = (((0, 1), (2, 3)), ((0, 1), (2, 3)), ((0, 1), (2,), (3,)))
 
 
 def tile_picked_yskrig_est_p_kernel(tc, x_words, x_scales, w1, h1, h2, rho, unit, w2, offs, n1, n2, out):
     nc = tc.nc
     with ExitStack() as ctx:
         sb = ctx.enter_context(tc.tile_pool(name="sb", bufs=1))
-        rot = ctx.enter_context(tc.psum_pool(name="rot", bufs=4))
+        rot = ctx.enter_context(tc.psum_pool(name="rot", bufs=2))
         acc = ctx.enter_context(tc.psum_pool(name="acc", bufs=1))
 
         offs_sb = sb.tile([P, S // 16], U16, name="offs_sb")
@@ -39,28 +37,29 @@ def tile_picked_yskrig_est_p_kernel(tc, x_words, x_scales, w1, h1, h2, rho, unit
         ident = sb.tile([P, P], F32, name="ident")
         make_identity(nc, ident[:])
 
-        hs = [sb.tile([P, 2, S], F32, name="h_%d" % (t,)) for t in range(NT)]
+        hs = [[sb.tile([P, S], F32, name="h_%d_%d" % (t, l), align_bytes=64) for l in range(2)] for t in range(NT)]
         rh = [sb.tile([P, S], F32, name="rho_%d" % (t,)) for t in range(NT)]
         w1_raw = sb.tile([P, 4, H], F32, name="w1_raw")
         w2_raw = sb.tile([P, 4, N], F32, name="w2_raw")
         unit_sb = sb.tile([P, NT], F32, name="unit_sb")
 
+        def dealt(src, t):
+            return src.rearrange("(p t) j -> p t j", t=NT)[:, t, :]
+
         def load_rows(t):
-            rows = slice(t * P, (t + 1) * P)
-            nc.sync.dma_start(hs[t][:, 1, :], h2[rows, :])
+            nc.sync.dma_start(hs[t][1][:], dealt(h2, t))
             if t == 0:
-                nc.sync.dma_start(rh[t][:], rho[rows, :])
-            nc.sync.dma_start(hs[t][:, 0, :], h1[rows, :])
+                nc.sync.dma_start(rh[t][:], dealt(rho, t))
+            nc.sync.dma_start(hs[t][0][:], dealt(h1, t))
             if t > 0:
-                nc.sync.dma_start(rh[t][:], rho[rows, :])
+                nc.sync.dma_start(rh[t][:], dealt(rho, t))
 
         def load_x():
             nc.sync.dma_start(xw[:], x_words[0].rearrange("p n t -> p (n t)").bitcast(I32))
 
         def load_w1():
             nc.sync.dma_start(w1_raw[:], w1.rearrange("(p j) c -> p j c", j=4))
-            with nc.allow_non_contiguous_dma(reason="one value a partition and row tile"):
-                nc.sync.dma_start(unit_sb[:], unit.rearrange("(t p) o -> p (t o)", p=P))
+            nc.sync.dma_start(unit_sb[:], unit.rearrange("(p t) o -> p (t o)", t=NT))
             nc.sync.dma_start(n_sb[0][:], n1)
             nc.sync.dma_start(n_sb[1][:], n2)
 
@@ -68,11 +67,11 @@ def tile_picked_yskrig_est_p_kernel(tc, x_words, x_scales, w1, h1, h2, rho, unit
         for q in range(4):
             nc.sync.dma_start(xs[32 * q : 32 * q + 32, :].bitcast(I32), x_scales[0, 4 * q : 4 * q + 4, :].bitcast(I32).partition_broadcast(8))
         load_rows(0)
-        load_rows(1)
         load_x()
+        load_rows(1)
+        load_w1()
         load_rows(2)
         load_rows(3)
-        load_w1()
         nc.sync.dma_start(w2_raw[:], w2.rearrange("(p j) c -> p j c", j=4))
 
         gw = sb.tile([P, S], U32, name="gw", align_bytes=64)
@@ -83,24 +82,32 @@ def tile_picked_yskrig_est_p_kernel(tc, x_words, x_scales, w1, h1, h2, rho, unit
         cs = [sb.tile([P, 2, S], F32, name="c_%d" % (t,)) for t in range(NT)]
         ms = [sb.tile([P, 2, S], F32, name="m_%d" % (t,)) for t in range(NT)]
         ws = sb.tile([P, NT, 2, S], F32, name="ws")
-        sq = sb.tile([P, 4, NT, P], F32, name="sq")
-        d2 = sb.tile([P, 4, NT, P], F32, name="d2")
+        sq = sb.tile([P, NT, S], F32, name="sq")
+        d2 = sb.tile([P, 4, 2, P, 2], F32, name="d2")
 
         def weights(t):
             if t == 0:
                 for l in (1, 0):
-                    nc.scalar.activation(cs[t][:, l, :], hs[t][:, l, :], ACT.Exp, scale=-1.0)
+                    nc.scalar.activation(cs[t][:, l, :], hs[t][l][:], ACT.Exp, scale=-1.0)
                     nc.vector.tensor_tensor(ms[t][:, 1 - l, :], rh[t][:], cs[t][:, l, :], ALU.mult)
                 nc.vector.tensor_tensor(ws[:, t, :, :], cs[t][:], ms[t][:], ALU.subtract)
             else:
-                nc.scalar.activation(cs[t][:], hs[t][:], ACT.Exp, scale=-1.0)
+                for l in (1, 0):
+                    nc.scalar.activation(cs[t][:, l, :], hs[t][l][:], ACT.Exp, scale=-1.0)
                 nc.vector.tensor_tensor(ms[t][:], rh[t][:].unsqueeze(1).to_broadcast([P, 2, S]), cs[t][:], ALU.mult)
                 nc.vector.tensor_tensor(ws[:, t, :, :], cs[t][:], ms[t][:, ::-1, :], ALU.subtract)
-            bank = rot.tile([P, 4, P], F32, name="bank")
-            for jb in range(4):
-                nc.tensor.transpose(bank[:, jb, :], rh[t][:, jb * P : (jb + 1) * P], ident[:])
-            nc.scalar.activation(sq[:, :, t, :], bank[:], ACT.Square)
-            nc.scalar.activation(d2[:, :, t, :], sq[:, :, t, :], ACT.Square, scale=-0.45, bias=0.525)
+            nc.scalar.activation(sq[:, t, :], rh[t][:], ACT.Square)
+            if t % 2 == 1:
+                u = t // 2
+                for g in range(2):
+                    bank = rot.tile([P, 2, 2, P], F32, name="bank")
+                    for b in range(2):
+                        for e in range(2):
+                            jb = 2 * g + b
+                            nc.tensor.transpose(bank[:, b, e, :], sq[:, 2 * u + e, jb * P : (jb + 1) * P], ident[:])
+                    half = 0.5 if g == 0 else 1.0
+                    nc.scalar.activation(d2[:, 2 * g : 2 * g + 2, u, :, :], bank[:].rearrange("p b e q -> p b q e"),
+                                         ACT.Square, scale=-0.9 * half, bias=1.05 * half)
 
         def side_by_side(dst, src):
             return dst.rearrange("p (c i) j -> p c j i", i=4), src.rearrange("p j (c i) -> p c j i", i=4)
@@ -108,91 +115,98 @@ def tile_picked_yskrig_est_p_kernel(tc, x_words, x_scales, w1, h1, h2, rho, unit
         w1b = sb.tile([P, H, 4], BF16, name="w1b", align_bytes=64)
         w1q = sb.tile([P, H], U32, name="w1q", align_bytes=64)
         w1s = sb.tile([P, H], U8, name="w1s", align_bytes=64)
-        y = [sb.tile([P, S], F32, name="y%d" % (t,)) for t in range(NT)]
+        y = []
 
         def first_product(t):
-            bank = rot.tile([P, S], F32, name="bank")
+            bank = rot.tile([P, S], F32, name="mxbank")
             cols = slice(t * P, (t + 1) * P)
             nc.tensor.matmul_mx(out=bank[:], lhsT=w1q[:, cols].bitcast(FP8X4), lhsT_scale=w1s[:, cols],
                                 rhs=gw[:].bitcast(FP8X4), rhs_scale=gs[:], start=True, stop=True)
+            y.append(sb.tile([P, S], F32, name="y%d" % (t,), tag=("h_3_%d" % (t,) if t < 2 else "y%d" % (t,)), align_bytes=64))
             nc.scalar.activation(y[t][:], bank[:], ACT.Copy, scale=unit_sb[:, t : t + 1])
+
+        def quantise_w1():
+            nc.vector.tensor_copy(w1b[:].rearrange("p (t m) j -> p m t j", t=NT), w1_raw[:].rearrange("p j (m t) -> p m t j", t=NT))
+            nc.vector.quantize_mx(out=w1q[:].bitcast(FP8X4), scales=w1s[:], in_=w1b[:].rearrange("p c j -> p (c j)"))
 
         weights(0)
         weights(1)
+        quantise_w1()
         weights(2)
         weights(3)
-        nc.vector.tensor_copy(*side_by_side(w1b[:], w1_raw[:]))
-        nc.vector.quantize_mx(out=w1q[:].bitcast(FP8X4), scales=w1s[:], in_=w1b[:].rearrange("p c j -> p (c j)"))
-        first_product(0)
-        first_product(1)
-        first_product(2)
-        first_product(3)
+        for t in range(NT):
+            first_product(t)
 
-        w2b = sb.tile([P, N, 4], BF16, name="w2b", align_bytes=64)
-        w2q = sb.tile([P, N], U32, name="w2q", align_bytes=64)
-        w2s = sb.tile([P, N], U8, name="w2s", align_bytes=64)
-
-        inv = sb.tile([P, 4, H], F32, name="inv")
-        sgn = sb.tile([P, 4, H], BF16, name="sgn")
-        sq3 = sq[:].rearrange("p b t q -> p b (t q)")
-        d23 = d2[:].rearrange("p b t q -> p b (t q)")
+        inv = [sb.tile([P, 2, H], F32, name="inv0", tag="unit_sb"), sb.tile([P, 2, H], F32, name="inv1")]
+        d23 = d2[:].rearrange("p b u q e -> p b (u q e)")
         sums = [acc.tile([P, NT, P], F32, name="sum%d" % (b,)) for b in range(4)]
-
-        rcp = sb.tile([P, H], F32, name="rcp")
-
-        def inverse(k):
-            j0, n = PIECES[k]
-            b = slice(j0 // P, (j0 + n) // P)
-            nc.scalar.activation(inv[:, b, :], d23[:, b, :], ACT.Abs_reciprocal_sqrt)
-            nc.vector.tensor_scalar(sgn[:, b, :], sq3[:, b, :], 1.05 / 0.9, 0.5, ALU.is_lt, ALU.subtract)
-            if k == len(PIECES) - 1:
-                nc.vector.tensor_tensor(rcp[:], inv[:, j0 // P, :], sgn[:, j0 // P, :], ALU.mult)
+        prs = {}
 
         def products(k):
             j0, n = PIECES[k]
             js = slice(j0, j0 + n)
             lc = slice(j0 // 16, (j0 + n) // 16)
-            for t0 in (0, 2):
-                ns = scalar_lists(k, t0)
-                pr = sb.tile([P, 2, 2, n], F32, name="p%d_%d" % (k, t0,))
+            prk = sb.tile([P, NT, 2, n], F32, name="p%d" % (k,), tag=("m_3", "c_3", "p2")[k])
+            prs[k] = prk
+            for ts in GROUPS[k]:
+                t0, nt = ts[0], len(ts)
+                ns = LISTS_ON_SCALAR[k][t0]
+                pr = prk[:, t0 : t0 + nt, :, :]
                 if ns:
-                    yg = sb.tile([P, 2, ns, n], F32, name="yg%d_%d" % (k, t0,))
+                    yg = sb.tile([P, nt, ns, n], F32, name="yg%d_%d" % (k, t0,))
                     for l in range(ns):
-                        for e in range(2):
+                        for e in range(nt):
                             nc.scalar.activation(yg[:, e, l, :], y[t0 + e][:].indirect(n_sb[l][:, lc]), ACT.Copy)
-                for e in range(2):
+                for e in range(nt):
                     for l in range(ns, 2):
                         nc.vector.tensor_tensor(pr[:, e, l, :], y[t0 + e][:].indirect(n_sb[l][:, lc]), ws[:, t0 + e, l, js], ALU.mult)
                 if ns:
-                    nc.vector.tensor_tensor(pr[:, :, 0:ns, :], yg[:], ws[:, t0 : t0 + 2, 0:ns, js], ALU.mult)
-                for e in range(2):
+                    nc.vector.tensor_tensor(pr[:, :, 0:ns, :], yg[:], ws[:, t0 : t0 + nt, 0:ns, js], ALU.mult)
+                for e in range(nt):
                     for b in range(n // P):
                         for l in range(2):
                             nc.tensor.matmul(sums[j0 // P + b][:, t0 + e, :], pr[:, e, l, b * P : (b + 1) * P], ident[:],
                                              is_transpose=True, start=(l == 0), stop=(l == 1))
+            b = slice(j0 // P, (j0 + n) // P)
+            nc.scalar.activation(inv[b.start // 2][:, b.start % 2 : b.start % 2 + n // P, :], d23[:, b, :], ACT.Abs_reciprocal_sqrt)
+
+        sgn = [sb.tile([P, S // 2, NT], BF16, name="sgn0")]
+        products(0)
+        nc.vector.tensor_scalar(*side_by_side(sgn[0][:], sq[:, :, 0 : S // 2]), 1.05 / 0.9, 0.5, ALU.is_lt, ALU.subtract)
+        products(1)
+        products(2)
+
+        w2b = sb.tile([P, N, 4], BF16, name="w2b", tag="y2", align_bytes=64)
+        w2q = sb.tile([P, N], U32, name="w2q", align_bytes=64)
+        w2s = sb.tile([P, N], U8, name="w2s", align_bytes=64)
+        nc.scalar.copy(*side_by_side(w2b[:], w2_raw[:]))
+        nc.vector.quantize_mx(out=w2q[:].bitcast(FP8X4), scales=w2s[:], in_=w2b[:].rearrange("p c j -> p (c j)"))
+        sgn.append(sb.tile([P, S // 2, NT], BF16, name="sgn1", tag="y3", align_bytes=64))
+        nc.scalar.activation(*side_by_side(sgn[1][:], sq[:, :, S // 2 : S]), ACT.Sign, scale=-0.9, bias=1.05)
 
         def finish(k):
             j0, n = PIECES[k]
             nb = n // P
-            hid_t = sb.tile([P, nb, H], BF16, name="hid_t%d" % (j0,))
-            if k == len(PIECES) - 1:
-                nc.vector.tensor_tensor(hid_t[:, 0, :], sums[j0 // P][:].rearrange("p t q -> p (t q)"), rcp[:], ALU.mult)
-            else:
-                mag = sb.tile([P, nb, H], BF16, name="mag%d" % (j0,))
-                for b in range(nb):
-                    nc.vector.tensor_tensor(mag[:, b, :], sums[j0 // P + b][:].rearrange("p t q -> p (t q)"), inv[:, j0 // P + b, :], ALU.mult)
-                nc.vector.tensor_tensor(hid_t[:], mag[:], sgn[:, j0 // P : j0 // P + nb, :], ALU.mult)
+            mag = sb.tile([P, nb, H], BF16, name="mag%d" % (j0,))
             back = rot.tile([P, nb, 2, P], F32, name="bank")
-            for b in range(nb):
-                words = hid_t[:, b, :].bitcast(F32)
-                for u in range(2):
-                    nc.tensor.transpose(back[:, b, u, :], words[:, u : H // 2 : 2], ident[:])
             hid = sb.tile([P, n * 4], BF16, name="hid%d" % (j0,), align_bytes=64)
-            nc.scalar.copy(hid[:].bitcast(F32).rearrange("p (b j u) -> p b j u", b=nb, u=2), back[:].rearrange("p b u j -> p b j u"))
+            for b in range(nb):
+                nc.vector.tensor_tensor(mag[:, b, :].rearrange("p (u q e) -> p u q e", u=2, e=2),
+                                        sums[j0 // P + b][:].rearrange("p (u e) q -> p u q e", e=2),
+                                        inv[(j0 // P + b) // 2][:, (j0 // P + b) % 2, :].rearrange("p (u q e) -> p u q e", u=2, e=2), ALU.mult)
+            for b in range(nb):
+                words = mag[:, b, :].bitcast(F32)
+                for u in range(2):
+                    nc.tensor.transpose(back[:, b, u, :], words[:, u * P : (u + 1) * P], ident[:])
+            for b in range(nb):
+                jb = j0 // P + b
+                nc.vector.tensor_tensor(hid[:, b * H : (b + 1) * H].rearrange("p (j u e) -> p j u e", u=2, e=2),
+                                        back[:, b, :, :].bitcast(BF16).rearrange("p u (j e) -> p j u e", e=2),
+                                        sgn[jb // 2][:, (jb % 2) * P : (jb % 2 + 1) * P, :].rearrange("p j (u e) -> p j u e", e=2), ALU.mult)
             hq = sb.tile([P, n], U32, name="hq%d" % (j0,), align_bytes=64)
             hsc = sb.tile([P, n], U8, name="hsc%d" % (j0,), align_bytes=64)
             nc.vector.quantize_mx(out=hq[:].bitcast(FP8X4), scales=hsc[:], in_=hid[:])
-            bank = rot.tile([P, n], F32, name="bank")
+            bank = rot.tile([P, n], F32, name="mxbank")
             nc.tensor.matmul_mx(out=bank[:], lhsT=w2q[:].bitcast(FP8X4), lhsT_scale=w2s[:],
                                 rhs=hq[:].bitcast(FP8X4), rhs_scale=hsc[:], start=True, stop=True)
             res = sb.tile([P, n], F32, name="res%d" % (j0,))
@@ -200,11 +214,4 @@ def tile_picked_yskrig_est_p_kernel(tc, x_words, x_scales, w1, h1, h2, rho, unit
             nc.sync.dma_start(out[:, j0 : j0 + n], res[:])
 
         for k in range(len(PIECES)):
-            inverse(k)
-        products(0)
-        nc.scalar.copy(*side_by_side(w2b[:], w2_raw[:]))
-        nc.vector.quantize_mx(out=w2q[:].bitcast(FP8X4), scales=w2s[:], in_=w2b[:].rearrange("p c j -> p (c j)"))
-        for k in range(1, len(PIECES)):
-            products(k)
-            finish(k - 1)
-        finish(len(PIECES) - 1)
+            finish(k)

@@ -3,7 +3,7 @@ from contextlib import ExitStack
 import concourse.mybir as mybir
 from concourse.masks import make_identity
 
-FLOPS = 335544320
+FLOPS = 2 * 512 * 512 * 512 + 2 * 512 * 128 * 512
 
 F32 = mybir.dt.float32
 BF16 = mybir.dt.bfloat16
@@ -16,202 +16,208 @@ ALU = mybir.AluOpType
 ACT = mybir.ActivationFunctionType
 
 P = 128
-T, S, N, H = 1024, 512, 128, 512
-NT = H // P
-PIECES = ((0, 256), (256, 128), (384, 128))
-LISTS_ON_SCALAR = ((0, 0, 0, 0), (1, 1, 2, 2), (2, 2, 2, 2))
-GROUPS = (((0, 1), (2, 3)), ((0, 1), (2, 3)), ((0, 1), (2,), (3,)))
+PACK = 4
+STATIONS, TARGETS, HIDDEN, VARIABLES = 1024, 512, 512, 128
+HALF = TARGETS // 2
+PER_COLUMN = 16
+MX_ALIGN = 64
+RHO_FACTOR, PADDED_ONE = 0.9, 1.05
+
+PIECES = ((0, HALF), (HALF, P), (HALF + P, P))
+LAST = len(PIECES) - 1
+
+
+def lists_on_scalar(piece, t):
+    return int(piece > 0) + int(t >= 2)
+
+
+def row_groups(piece):
+    return ((0, 1), (2,), (3,)) if piece == LAST else ((0, 1), (2, 3))
+
+
+def side_by_side(dst, src):
+    return dst.rearrange("p (c i) r -> p c r i", i=4), src.rearrange("p r (c i) -> p c r i", i=4)
 
 
 def tile_picked_yskrig_est_p_kernel(tc, x_words, x_scales, w1, h1, h2, rho, unit, w2, offs, n1, n2, out):
     nc = tc.nc
     with ExitStack() as ctx:
         sb = ctx.enter_context(tc.tile_pool(name="sb", bufs=1))
-        rot = ctx.enter_context(tc.psum_pool(name="rot", bufs=2))
-        acc = ctx.enter_context(tc.psum_pool(name="acc", bufs=1))
+        turns = ctx.enter_context(tc.psum_pool(name="turns", bufs=2))
+        sums_pool = ctx.enter_context(tc.psum_pool(name="sums", bufs=1))
 
-        offs_sb = sb.tile([P, S // 16], U16, name="offs_sb")
-        n_sb = [sb.tile([P, S // 16], U16, name="n_sb%d" % (l,)) for l in range(2)]
-        xw = sb.tile([P, T], I32, name="xw", align_bytes=64)
-        xs = sb.tile([P, T], U8, name="xs", align_bytes=64)
+        offs_sb = sb.tile([P, TARGETS // PER_COLUMN], U16, name="offs_sb")
+        neighbours = [sb.tile([P, TARGETS // PER_COLUMN], U16, name="n%d_sb" % (l + 1,)) for l in range(2)]
+        x_word_table = sb.tile([P, STATIONS], I32, name="x_word_table", align_bytes=MX_ALIGN)
+        x_scale_table = sb.tile([P, STATIONS], U8, name="x_scale_table", align_bytes=MX_ALIGN)
         ident = sb.tile([P, P], F32, name="ident")
+        nc.gpsimd.memset(x_scale_table[:].bitcast(I32), 0)
         make_identity(nc, ident[:])
 
-        hs = [[sb.tile([P, S], F32, name="h_%d_%d" % (t, l), align_bytes=64) for l in range(2)] for t in range(NT)]
-        rh = [sb.tile([P, S], F32, name="rho_%d" % (t,)) for t in range(NT)]
-        w1_raw = sb.tile([P, 4, H], F32, name="w1_raw")
-        w2_raw = sb.tile([P, 4, N], F32, name="w2_raw")
-        unit_sb = sb.tile([P, NT], F32, name="unit_sb")
-
-        def dealt(src, t):
-            return src.rearrange("(p t) j -> p t j", t=NT)[:, t, :]
+        dist = [[sb.tile([P, TARGETS], F32, name="dist_%d_%d" % (t, l), align_bytes=MX_ALIGN) for l in range(2)]
+                for t in range(PACK)]
+        rho_sb = [sb.tile([P, TARGETS], F32, name="rho_%d" % (t,)) for t in range(PACK)]
+        w1_raw = sb.tile([P, PACK, HIDDEN], F32, name="w1_raw")
+        w2_raw = sb.tile([P, PACK, VARIABLES], F32, name="w2_raw")
+        unit_sb = sb.tile([P, PACK], F32, name="unit_sb")
 
         def load_rows(t):
-            nc.sync.dma_start(hs[t][1][:], dealt(h2, t))
-            if t == 0:
-                nc.sync.dma_start(rh[t][:], dealt(rho, t))
-            nc.sync.dma_start(hs[t][0][:], dealt(h1, t))
-            if t > 0:
-                nc.sync.dma_start(rh[t][:], dealt(rho, t))
+            loads = [(dist[t][1], h2), (dist[t][0], h1)]
+            loads.insert(1 if t == 0 else 2, (rho_sb[t], rho))
+            for dst, src in loads:
+                nc.sync.dma_start(dst[:], src.rearrange("(p t) j -> p t j", t=PACK)[:, t, :])
 
-        def load_x():
-            nc.sync.dma_start(xw[:], x_words[0].rearrange("p n t -> p (n t)").bitcast(I32))
-
-        def load_w1():
-            nc.sync.dma_start(w1_raw[:], w1.rearrange("(p j) c -> p j c", j=4))
-            nc.sync.dma_start(unit_sb[:], unit.rearrange("(p t) o -> p (t o)", t=NT))
-            nc.sync.dma_start(n_sb[0][:], n1)
-            nc.sync.dma_start(n_sb[1][:], n2)
-
-        nc.sync.dma_start(offs_sb[:], offs)
-        for q in range(4):
-            nc.sync.dma_start(xs[32 * q : 32 * q + 32, :].bitcast(I32), x_scales[0, 4 * q : 4 * q + 4, :].bitcast(I32).partition_broadcast(8))
         load_rows(0)
-        load_x()
+        nc.sync.dma_start(offs_sb[:], offs)
+        nc.sync.dma_start(x_word_table[:], x_words[0].rearrange("p n r -> p (n r)").bitcast(I32))
+        for q in range(4):
+            nc.sync.dma_start(x_scale_table[32 * q : 32 * q + 4, :].bitcast(I32),
+                              x_scales[0, 4 * q : 4 * q + 4, :].bitcast(I32))
         load_rows(1)
-        load_w1()
+        nc.sync.dma_start(w1_raw[:], w1.rearrange("(p r) c -> p r c", r=PACK))
+        nc.sync.dma_start(unit_sb[:], unit.rearrange("(p t) o -> p (t o)", t=PACK))
+        nc.sync.dma_start(neighbours[0][:], n1)
+        nc.sync.dma_start(neighbours[1][:], n2)
         load_rows(2)
         load_rows(3)
-        nc.sync.dma_start(w2_raw[:], w2.rearrange("(p j) c -> p j c", j=4))
+        nc.sync.dma_start(w2_raw[:], w2.rearrange("(p r) c -> p r c", r=PACK))
 
-        gw = sb.tile([P, S], U32, name="gw", align_bytes=64)
-        gs = sb.tile([P, S], U8, name="gs", align_bytes=64)
-        nc.vector.tensor_copy(gs[:], xs[:].indirect(offs_sb[:]))
-        nc.vector.tensor_copy(gw[:], xw[:].bitcast(U32).indirect(offs_sb[:]))
-
-        cs = [sb.tile([P, 2, S], F32, name="c_%d" % (t,)) for t in range(NT)]
-        ms = [sb.tile([P, 2, S], F32, name="m_%d" % (t,)) for t in range(NT)]
-        ws = sb.tile([P, NT, 2, S], F32, name="ws")
-        sq = sb.tile([P, NT, S], F32, name="sq")
-        d2 = sb.tile([P, 4, 2, P, 2], F32, name="d2")
+        x_codes = sb.tile([P, TARGETS], U32, name="x_codes", align_bytes=MX_ALIGN)
+        x_bytes = sb.tile([P, TARGETS], U8, name="x_bytes", align_bytes=MX_ALIGN)
+        cov = [sb.tile([P, 2, TARGETS], F32, name="cov_%d" % (t,)) for t in range(PACK)]
+        cross = [sb.tile([P, 2, TARGETS], F32, name="cross_%d" % (t,)) for t in range(PACK)]
+        weight = sb.tile([P, PACK, 2, TARGETS], F32, name="weight")
+        rho_sq = sb.tile([P, PACK, TARGETS], F32, name="rho_sq")
+        dn_sq = sb.tile([P, TARGETS // P, 2, P, 2], F32, name="dn_sq")
 
         def weights(t):
-            if t == 0:
-                for l in (1, 0):
-                    nc.scalar.activation(cs[t][:, l, :], hs[t][l][:], ACT.Exp, scale=-1.0)
-                    nc.vector.tensor_tensor(ms[t][:, 1 - l, :], rh[t][:], cs[t][:, l, :], ALU.mult)
-                nc.vector.tensor_tensor(ws[:, t, :, :], cs[t][:], ms[t][:], ALU.subtract)
-            else:
-                for l in (1, 0):
-                    nc.scalar.activation(cs[t][:, l, :], hs[t][l][:], ACT.Exp, scale=-1.0)
-                nc.vector.tensor_tensor(ms[t][:], rh[t][:].unsqueeze(1).to_broadcast([P, 2, S]), cs[t][:], ALU.mult)
-                nc.vector.tensor_tensor(ws[:, t, :, :], cs[t][:], ms[t][:, ::-1, :], ALU.subtract)
-            nc.scalar.activation(sq[:, t, :], rh[t][:], ACT.Square)
+            for l in (1, 0):
+                nc.scalar.activation(cov[t][:, l, :], dist[t][l][:], ACT.Exp, scale=-1.0)
+                nc.vector.tensor_tensor(cross[t][:, 1 - l, :], rho_sb[t][:], cov[t][:, l, :], ALU.mult)
+            for l in range(2):
+                nc.vector.tensor_tensor(weight[:, t, l, :], cov[t][:, l, :], cross[t][:, l, :], ALU.subtract)
+            nc.scalar.activation(rho_sq[:, t, :], rho_sb[t][:], ACT.Square)
             if t % 2 == 1:
                 u = t // 2
-                for g in range(2):
-                    bank = rot.tile([P, 2, 2, P], F32, name="bank")
+                for half in range(2):
+                    bank = turns.tile([P, 2, 2, P], F32, name="turn_bank")
                     for b in range(2):
                         for e in range(2):
-                            jb = 2 * g + b
-                            nc.tensor.transpose(bank[:, b, e, :], sq[:, 2 * u + e, jb * P : (jb + 1) * P], ident[:])
-                    half = 0.5 if g == 0 else 1.0
-                    nc.scalar.activation(d2[:, 2 * g : 2 * g + 2, u, :, :], bank[:].rearrange("p b e q -> p b q e"),
-                                         ACT.Square, scale=-0.9 * half, bias=1.05 * half)
+                            block = 2 * half + b
+                            nc.tensor.transpose(bank[:, b, e, :], rho_sq[:, 2 * u + e, block * P : (block + 1) * P], ident[:])
+                    size = 0.5 if half == 0 else 1.0
+                    nc.scalar.activation(dn_sq[:, 2 * half : 2 * half + 2, u, :, :], bank[:].rearrange("p b e q -> p b q e"),
+                                         ACT.Square, scale=-RHO_FACTOR * size, bias=PADDED_ONE * size)
 
-        def side_by_side(dst, src):
-            return dst.rearrange("p (c i) j -> p c j i", i=4), src.rearrange("p j (c i) -> p c j i", i=4)
-
-        w1b = sb.tile([P, H, 4], BF16, name="w1b", align_bytes=64)
-        w1q = sb.tile([P, H], U32, name="w1q", align_bytes=64)
-        w1s = sb.tile([P, H], U8, name="w1s", align_bytes=64)
+        w1_bf = [sb.tile([P, HIDDEN // 2, PACK], BF16, name="w1_bf%d" % (g,), align_bytes=MX_ALIGN) for g in range(2)]
+        w1_codes = sb.tile([P, HIDDEN], U32, name="w1_codes", align_bytes=MX_ALIGN)
+        w1_bytes = sb.tile([P, HIDDEN], U8, name="w1_bytes", align_bytes=MX_ALIGN)
         y = []
 
+        def quantise_w1():
+            for g in range(2):
+                nc.vector.tensor_copy(w1_bf[g][:].rearrange("p (t m) r -> p m t r", t=2),
+                                      w1_raw[:].rearrange("p r (m t) -> p m t r", t=PACK)[:, :, 2 * g : 2 * g + 2, :])
+            for g in range(2):
+                cols = slice(g * HIDDEN // 2, (g + 1) * HIDDEN // 2)
+                nc.vector.quantize_mx(out=w1_codes[:, cols].bitcast(FP8X4), scales=w1_bytes[:, cols],
+                                      in_=w1_bf[g][:].rearrange("p c r -> p (c r)"))
+
         def first_product(t):
-            bank = rot.tile([P, S], F32, name="mxbank")
+            bank = turns.tile([P, TARGETS], F32, name="mx_bank")
             cols = slice(t * P, (t + 1) * P)
-            nc.tensor.matmul_mx(out=bank[:], lhsT=w1q[:, cols].bitcast(FP8X4), lhsT_scale=w1s[:, cols],
-                                rhs=gw[:].bitcast(FP8X4), rhs_scale=gs[:], start=True, stop=True)
-            y.append(sb.tile([P, S], F32, name="y%d" % (t,), tag=("h_3_%d" % (t,) if t < 2 else "y%d" % (t,)), align_bytes=64))
+            nc.tensor.matmul_mx(out=bank[:], lhsT=w1_codes[:, cols].bitcast(FP8X4), lhsT_scale=w1_bytes[:, cols],
+                                rhs=x_codes[:].bitcast(FP8X4), rhs_scale=x_bytes[:], start=True, stop=True)
+            tag = "dist_%d_%d" % (PACK - 1, t) if t < 2 else "y%d" % (t,)
+            y.append(sb.tile([P, TARGETS], F32, name="y%d" % (t,), tag=tag, align_bytes=MX_ALIGN))
             nc.scalar.activation(y[t][:], bank[:], ACT.Copy, scale=unit_sb[:, t : t + 1])
 
-        def quantise_w1():
-            nc.vector.tensor_copy(w1b[:].rearrange("p (t m) j -> p m t j", t=NT), w1_raw[:].rearrange("p j (m t) -> p m t j", t=NT))
-            nc.vector.quantize_mx(out=w1q[:].bitcast(FP8X4), scales=w1s[:], in_=w1b[:].rearrange("p c j -> p (c j)"))
-
         weights(0)
+        nc.vector.tensor_copy(x_codes[:], x_word_table[:].bitcast(U32).indirect(offs_sb[:]))
+        nc.vector.tensor_copy(x_bytes[:], x_scale_table[:].indirect(offs_sb[:]))
         weights(1)
         quantise_w1()
         weights(2)
         weights(3)
-        for t in range(NT):
+        for t in range(PACK):
             first_product(t)
 
-        inv = [sb.tile([P, 2, H], F32, name="inv0", tag="unit_sb"), sb.tile([P, 2, H], F32, name="inv1")]
-        d23 = d2[:].rearrange("p b u q e -> p b (u q e)")
-        sums = [acc.tile([P, NT, P], F32, name="sum%d" % (b,)) for b in range(4)]
-        prs = {}
+        inv = [sb.tile([P, 2, HIDDEN], F32, name="inv0", tag="unit_sb"), sb.tile([P, 2, HIDDEN], F32, name="inv1")]
+        sums = [sums_pool.tile([P, PACK, P], F32, name="sum%d" % (block,)) for block in range(TARGETS // P)]
+        product_tags = ("cross_%d" % (PACK - 1,), "cov_%d" % (PACK - 1,), "products_last")
 
-        def products(k):
-            j0, n = PIECES[k]
-            js = slice(j0, j0 + n)
-            lc = slice(j0 // 16, (j0 + n) // 16)
-            prk = sb.tile([P, NT, 2, n], F32, name="p%d" % (k,), tag=("m_3", "c_3", "p2")[k])
-            prs[k] = prk
-            for ts in GROUPS[k]:
-                t0, nt = ts[0], len(ts)
-                ns = LISTS_ON_SCALAR[k][t0]
-                pr = prk[:, t0 : t0 + nt, :, :]
-                if ns:
-                    yg = sb.tile([P, nt, ns, n], F32, name="yg%d_%d" % (k, t0,))
-                    for l in range(ns):
-                        for e in range(nt):
-                            nc.scalar.activation(yg[:, e, l, :], y[t0 + e][:].indirect(n_sb[l][:, lc]), ACT.Copy)
-                for e in range(nt):
-                    for l in range(ns, 2):
-                        nc.vector.tensor_tensor(pr[:, e, l, :], y[t0 + e][:].indirect(n_sb[l][:, lc]), ws[:, t0 + e, l, js], ALU.mult)
-                if ns:
-                    nc.vector.tensor_tensor(pr[:, :, 0:ns, :], yg[:], ws[:, t0 : t0 + nt, 0:ns, js], ALU.mult)
-                for e in range(nt):
+        def products(piece):
+            j0, n = PIECES[piece]
+            targets = slice(j0, j0 + n)
+            entries = slice(j0 // PER_COLUMN, (j0 + n) // PER_COLUMN)
+            prod = sb.tile([P, PACK, 2, n], F32, name="prod%d" % (piece,), tag=product_tags[piece])
+            for group in row_groups(piece):
+                t0, t1 = group[0], group[-1] + 1
+                on_scalar = lists_on_scalar(piece, t0)
+                if on_scalar:
+                    picked = sb.tile([P, len(group), on_scalar, n], F32, name="picked%d_%d" % (piece, t0))
+                    for l in range(on_scalar):
+                        for t in group:
+                            nc.scalar.activation(picked[:, t - t0, l, :], y[t][:].indirect(neighbours[l][:, entries]), ACT.Copy)
+                for t in group:
+                    for l in range(on_scalar, 2):
+                        nc.vector.tensor_tensor(prod[:, t, l, :], y[t][:].indirect(neighbours[l][:, entries]),
+                                                weight[:, t, l, targets], ALU.mult)
+                if on_scalar:
+                    nc.vector.tensor_tensor(prod[:, t0:t1, 0:on_scalar, :], picked[:],
+                                            weight[:, t0:t1, 0:on_scalar, targets], ALU.mult)
+                for t in group:
                     for b in range(n // P):
                         for l in range(2):
-                            nc.tensor.matmul(sums[j0 // P + b][:, t0 + e, :], pr[:, e, l, b * P : (b + 1) * P], ident[:],
+                            nc.tensor.matmul(sums[j0 // P + b][:, t, :], prod[:, t, l, b * P : (b + 1) * P], ident[:],
                                              is_transpose=True, start=(l == 0), stop=(l == 1))
-            b = slice(j0 // P, (j0 + n) // P)
-            nc.scalar.activation(inv[b.start // 2][:, b.start % 2 : b.start % 2 + n // P, :], d23[:, b, :], ACT.Abs_reciprocal_sqrt)
+            first = j0 // P
+            nc.scalar.activation(inv[first // 2][:, first % 2 : first % 2 + n // P, :],
+                                 dn_sq[:, first : first + n // P].rearrange("p b u q e -> p b (u q e)"), ACT.Abs_reciprocal_sqrt)
 
-        sgn = [sb.tile([P, S // 2, NT], BF16, name="sgn0")]
+        sign = [sb.tile([P, HALF, PACK], BF16, name="sign0")]
         products(0)
-        nc.vector.tensor_scalar(*side_by_side(sgn[0][:], sq[:, :, 0 : S // 2]), 1.05 / 0.9, 0.5, ALU.is_lt, ALU.subtract)
+        nc.vector.tensor_scalar(*side_by_side(sign[0][:], rho_sq[:, :, 0:HALF]), PADDED_ONE / RHO_FACTOR, 0.5,
+                                ALU.is_lt, ALU.subtract)
         products(1)
-        products(2)
+        products(LAST)
 
-        w2b = sb.tile([P, N, 4], BF16, name="w2b", tag="y2", align_bytes=64)
-        w2q = sb.tile([P, N], U32, name="w2q", align_bytes=64)
-        w2s = sb.tile([P, N], U8, name="w2s", align_bytes=64)
-        nc.scalar.copy(*side_by_side(w2b[:], w2_raw[:]))
-        nc.vector.quantize_mx(out=w2q[:].bitcast(FP8X4), scales=w2s[:], in_=w2b[:].rearrange("p c j -> p (c j)"))
-        sgn.append(sb.tile([P, S // 2, NT], BF16, name="sgn1", tag="y3", align_bytes=64))
-        nc.scalar.activation(*side_by_side(sgn[1][:], sq[:, :, S // 2 : S]), ACT.Sign, scale=-0.9, bias=1.05)
+        w2_bf = sb.tile([P, VARIABLES, PACK], BF16, name="w2_bf", tag="y2", align_bytes=MX_ALIGN)
+        w2_codes = sb.tile([P, VARIABLES], U32, name="w2_codes", align_bytes=MX_ALIGN)
+        w2_bytes = sb.tile([P, VARIABLES], U8, name="w2_bytes", align_bytes=MX_ALIGN)
+        nc.scalar.copy(*side_by_side(w2_bf[:], w2_raw[:]))
+        nc.vector.quantize_mx(out=w2_codes[:].bitcast(FP8X4), scales=w2_bytes[:], in_=w2_bf[:].rearrange("p c r -> p (c r)"))
+        sign.append(sb.tile([P, HALF, PACK], BF16, name="sign1", tag="y3", align_bytes=MX_ALIGN))
+        nc.scalar.activation(*side_by_side(sign[1][:], rho_sq[:, :, HALF:TARGETS]), ACT.Sign, scale=-RHO_FACTOR, bias=PADDED_ONE)
 
-        def finish(k):
-            j0, n = PIECES[k]
-            nb = n // P
-            mag = sb.tile([P, nb, H], BF16, name="mag%d" % (j0,))
-            back = rot.tile([P, nb, 2, P], F32, name="bank")
-            hid = sb.tile([P, n * 4], BF16, name="hid%d" % (j0,), align_bytes=64)
-            for b in range(nb):
-                nc.vector.tensor_tensor(mag[:, b, :].rearrange("p (u q e) -> p u q e", u=2, e=2),
-                                        sums[j0 // P + b][:].rearrange("p (u e) q -> p u q e", e=2),
-                                        inv[(j0 // P + b) // 2][:, (j0 // P + b) % 2, :].rearrange("p (u q e) -> p u q e", u=2, e=2), ALU.mult)
-            for b in range(nb):
-                words = mag[:, b, :].bitcast(F32)
+        def finish(piece):
+            j0, n = PIECES[piece]
+            blocks = range(j0 // P, (j0 + n) // P)
+            unsigned = sb.tile([P, len(blocks), HIDDEN], BF16, name="unsigned%d" % (piece,))
+            bank = turns.tile([P, len(blocks), 2, P], F32, name="turn_bank")
+            hid = sb.tile([P, n * PACK], BF16, name="hid%d" % (piece,), align_bytes=MX_ALIGN)
+            for b, block in enumerate(blocks):
+                nc.vector.tensor_tensor(unsigned[:, b, :].rearrange("p (u q e) -> p u q e", u=2, e=2),
+                                        sums[block][:].rearrange("p (u e) q -> p u q e", e=2),
+                                        inv[block // 2][:, block % 2, :].rearrange("p (u q e) -> p u q e", u=2, e=2), ALU.mult)
+            for b in range(len(blocks)):
+                words = unsigned[:, b, :].bitcast(F32)
                 for u in range(2):
-                    nc.tensor.transpose(back[:, b, u, :], words[:, u * P : (u + 1) * P], ident[:])
-            for b in range(nb):
-                jb = j0 // P + b
-                nc.vector.tensor_tensor(hid[:, b * H : (b + 1) * H].rearrange("p (j u e) -> p j u e", u=2, e=2),
-                                        back[:, b, :, :].bitcast(BF16).rearrange("p u (j e) -> p j u e", e=2),
-                                        sgn[jb // 2][:, (jb % 2) * P : (jb % 2 + 1) * P, :].rearrange("p j (u e) -> p j u e", e=2), ALU.mult)
-            hq = sb.tile([P, n], U32, name="hq%d" % (j0,), align_bytes=64)
-            hsc = sb.tile([P, n], U8, name="hsc%d" % (j0,), align_bytes=64)
-            nc.vector.quantize_mx(out=hq[:].bitcast(FP8X4), scales=hsc[:], in_=hid[:])
-            bank = rot.tile([P, n], F32, name="mxbank")
-            nc.tensor.matmul_mx(out=bank[:], lhsT=w2q[:].bitcast(FP8X4), lhsT_scale=w2s[:],
-                                rhs=hq[:].bitcast(FP8X4), rhs_scale=hsc[:], start=True, stop=True)
-            res = sb.tile([P, n], F32, name="res%d" % (j0,))
-            nc.scalar.copy(res[:], bank[:])
-            nc.sync.dma_start(out[:, j0 : j0 + n], res[:])
+                    nc.tensor.transpose(bank[:, b, u, :], words[:, u * P : (u + 1) * P], ident[:])
+            for b, block in enumerate(blocks):
+                nc.vector.tensor_tensor(hid[:, b * HIDDEN : (b + 1) * HIDDEN].rearrange("p (j u e) -> p j u e", u=2, e=2),
+                                        bank[:, b, :, :].bitcast(BF16).rearrange("p u (j e) -> p j u e", e=2),
+                                        sign[block // 2][:, (block % 2) * P : (block % 2 + 1) * P, :].rearrange(
+                                            "p j (u e) -> p j u e", e=2), ALU.mult)
+            hid_codes = sb.tile([P, n], U32, name="hid_codes%d" % (piece,), align_bytes=MX_ALIGN)
+            hid_bytes = sb.tile([P, n], U8, name="hid_bytes%d" % (piece,), align_bytes=MX_ALIGN)
+            nc.vector.quantize_mx(out=hid_codes[:].bitcast(FP8X4), scales=hid_bytes[:], in_=hid[:])
+            result_bank = turns.tile([P, n], F32, name="mx_bank")
+            nc.tensor.matmul_mx(out=result_bank[:], lhsT=w2_codes[:].bitcast(FP8X4), lhsT_scale=w2_bytes[:],
+                                rhs=hid_codes[:].bitcast(FP8X4), rhs_scale=hid_bytes[:], start=True, stop=True)
+            result = sb.tile([P, n], F32, name="result%d" % (piece,))
+            nc.scalar.copy(result[:], result_bank[:])
+            nc.sync.dma_start(out[:, j0 : j0 + n], result[:])
 
-        for k in range(len(PIECES)):
-            finish(k)
+        for piece in range(len(PIECES)):
+            finish(piece)

@@ -176,17 +176,17 @@ def tile_picked_yskrig_est_p_kernel(tc, x_words, x_scales, w1, h1, h2, rho, unit
                                  dn_sq[:, first : first + n // P].rearrange("p b u q e -> p b (u q e)"), ACT.Abs_reciprocal_sqrt)
 
         sign = [sb.tile([P, HALF, PACK], BF16, name="sign0")]
+        w2_bf = sb.tile([P, VARIABLES, PACK], BF16, name="w2_bf", align_bytes=MX_ALIGN)
+        w2_codes = sb.tile([P, VARIABLES], U32, name="w2_codes", align_bytes=MX_ALIGN)
+        w2_bytes = sb.tile([P, VARIABLES], U8, name="w2_bytes", align_bytes=MX_ALIGN)
         products(0)
+        nc.vector.tensor_copy(*side_by_side(w2_bf[:], w2_raw[:]))
         nc.vector.tensor_scalar(*side_by_side(sign[0][:], rho_sq[:, :, 0:HALF]), PADDED_ONE / RHO_FACTOR, 0.5,
                                 ALU.is_lt, ALU.subtract)
+        nc.vector.quantize_mx(out=w2_codes[:].bitcast(FP8X4), scales=w2_bytes[:], in_=w2_bf[:].rearrange("p c r -> p (c r)"))
         products(1)
         products(LAST)
 
-        w2_bf = sb.tile([P, VARIABLES, PACK], BF16, name="w2_bf", tag="y2", align_bytes=MX_ALIGN)
-        w2_codes = sb.tile([P, VARIABLES], U32, name="w2_codes", align_bytes=MX_ALIGN)
-        w2_bytes = sb.tile([P, VARIABLES], U8, name="w2_bytes", align_bytes=MX_ALIGN)
-        nc.scalar.copy(*side_by_side(w2_bf[:], w2_raw[:]))
-        nc.vector.quantize_mx(out=w2_codes[:].bitcast(FP8X4), scales=w2_bytes[:], in_=w2_bf[:].rearrange("p c r -> p (c r)"))
         sign.append(sb.tile([P, HALF, PACK], BF16, name="sign1", tag="y3", align_bytes=MX_ALIGN))
         nc.scalar.activation(*side_by_side(sign[1][:], rho_sq[:, :, HALF:TARGETS]), ACT.Sign, scale=-RHO_FACTOR, bias=PADDED_ONE)
 

from contextlib import ExitStack

import concourse.mybir as mybir
from concourse.masks import make_identity

FLOPS = 2 * 512 * 512 * 512 + 2 * 512 * 128 * 512

F32 = mybir.dt.float32
BF16 = mybir.dt.bfloat16
I32 = mybir.dt.int32
U32 = mybir.dt.uint32
U16 = mybir.dt.uint16
U8 = mybir.dt.uint8
FP8X4 = mybir.dt.float8_e4m3fn_x4
ALU = mybir.AluOpType
ACT = mybir.ActivationFunctionType

P = 128
PACK = 4
STATIONS, TARGETS, HIDDEN, VARIABLES = 1024, 512, 512, 128
HALF = TARGETS // 2
PER_COLUMN = 16
MX_ALIGN = 64
RHO_FACTOR, PADDED_ONE = 0.9, 1.05

PIECES = ((0, HALF), (HALF, P), (HALF + P, P))
LAST = len(PIECES) - 1


def lists_on_scalar(piece, t):
    return int(piece > 0) + int(t >= 2)


def row_groups(piece):
    return ((0, 1), (2,), (3,)) if piece == LAST else ((0, 1), (2, 3))


def side_by_side(dst, src):
    return dst.rearrange("p (c i) r -> p c r i", i=4), src.rearrange("p r (c i) -> p c r i", i=4)


def tile_picked_yskrig_est_p_kernel(tc, x_words, x_scales, w1, h1, h2, rho, unit, w2, offs, n1, n2, out):
    nc = tc.nc
    with ExitStack() as ctx:
        sb = ctx.enter_context(tc.tile_pool(name="sb", bufs=1))
        turns = ctx.enter_context(tc.psum_pool(name="turns", bufs=2))
        sums_pool = ctx.enter_context(tc.psum_pool(name="sums", bufs=1))

        offs_sb = sb.tile([P, TARGETS // PER_COLUMN], U16, name="offs_sb")
        neighbours = [sb.tile([P, TARGETS // PER_COLUMN], U16, name="n%d_sb" % (l + 1,)) for l in range(2)]
        x_word_table = sb.tile([P, STATIONS], I32, name="x_word_table", align_bytes=MX_ALIGN)
        x_scale_table = sb.tile([P, STATIONS], U8, name="x_scale_table", align_bytes=MX_ALIGN)
        ident = sb.tile([P, P], F32, name="ident")
        nc.gpsimd.memset(x_scale_table[:].bitcast(I32), 0)
        make_identity(nc, ident[:])

        dist = [[sb.tile([P, TARGETS], F32, name="dist_%d_%d" % (t, l), align_bytes=MX_ALIGN) for l in range(2)]
                for t in range(PACK)]
        rho_sb = [sb.tile([P, TARGETS], F32, name="rho_%d" % (t,)) for t in range(PACK)]
        w1_raw = sb.tile([P, PACK, HIDDEN], F32, name="w1_raw")
        w2_raw = sb.tile([P, PACK, VARIABLES], F32, name="w2_raw")
        unit_sb = sb.tile([P, PACK], F32, name="unit_sb")

        def load_rows(t):
            loads = [(dist[t][1], h2), (dist[t][0], h1)]
            loads.insert(1 if t == 0 else 2, (rho_sb[t], rho))
            for dst, src in loads:
                nc.sync.dma_start(dst[:], src.rearrange("(p t) j -> p t j", t=PACK)[:, t, :])

        load_rows(0)
        nc.sync.dma_start(offs_sb[:], offs)
        nc.sync.dma_start(x_word_table[:], x_words[0].rearrange("p n r -> p (n r)").bitcast(I32))
        for q in range(4):
            nc.sync.dma_start(x_scale_table[32 * q : 32 * q + 4, :].bitcast(I32),
                              x_scales[0, 4 * q : 4 * q + 4, :].bitcast(I32))
        load_rows(1)
        nc.sync.dma_start(w1_raw[:], w1.rearrange("(p r) c -> p r c", r=PACK))
        nc.sync.dma_start(unit_sb[:], unit.rearrange("(p t) o -> p (t o)", t=PACK))
        nc.sync.dma_start(neighbours[0][:], n1)
        nc.sync.dma_start(neighbours[1][:], n2)
        load_rows(2)
        load_rows(3)
        nc.sync.dma_start(w2_raw[:], w2.rearrange("(p r) c -> p r c", r=PACK))

        x_codes = sb.tile([P, TARGETS], U32, name="x_codes", align_bytes=MX_ALIGN)
        x_bytes = sb.tile([P, TARGETS], U8, name="x_bytes", align_bytes=MX_ALIGN)
        cov = [sb.tile([P, 2, TARGETS], F32, name="cov_%d" % (t,)) for t in range(PACK)]
        cross = [sb.tile([P, 2, TARGETS], F32, name="cross_%d" % (t,)) for t in range(PACK)]
        weight = sb.tile([P, PACK, 2, TARGETS], F32, name="weight")
        rho_sq = sb.tile([P, PACK, TARGETS], F32, name="rho_sq")
        dn_sq = sb.tile([P, TARGETS // P, 2, P, 2], F32, name="dn_sq")

        def weights(t):
            for l in (1, 0):
                nc.scalar.activation(cov[t][:, l, :], dist[t][l][:], ACT.Exp, scale=-1.0)
                nc.vector.tensor_tensor(cross[t][:, 1 - l, :], rho_sb[t][:], cov[t][:, l, :], ALU.mult)
            for l in range(2):
                nc.vector.tensor_tensor(weight[:, t, l, :], cov[t][:, l, :], cross[t][:, l, :], ALU.subtract)
            nc.scalar.activation(rho_sq[:, t, :], rho_sb[t][:], ACT.Square)
            if t % 2 == 1:
                u = t // 2
                for half in range(2):
                    bank = turns.tile([P, 2, 2, P], F32, name="turn_bank")
                    for b in range(2):
                        for e in range(2):
                            block = 2 * half + b
                            nc.tensor.transpose(bank[:, b, e, :], rho_sq[:, 2 * u + e, block * P : (block + 1) * P], ident[:])
                    size = 0.5 if half == 0 else 1.0
                    nc.scalar.activation(dn_sq[:, 2 * half : 2 * half + 2, u, :, :], bank[:].rearrange("p b e q -> p b q e"),
                                         ACT.Square, scale=-RHO_FACTOR * size, bias=PADDED_ONE * size)

        w1_bf = [sb.tile([P, HIDDEN // 2, PACK], BF16, name="w1_bf%d" % (g,), align_bytes=MX_ALIGN) for g in range(2)]
        w1_codes = sb.tile([P, HIDDEN], U32, name="w1_codes", align_bytes=MX_ALIGN)
        w1_bytes = sb.tile([P, HIDDEN], U8, name="w1_bytes", align_bytes=MX_ALIGN)
        y = []

        def quantise_w1():
            for g in range(2):
                nc.vector.tensor_copy(w1_bf[g][:].rearrange("p (t m) r -> p m t r", t=2),
                                      w1_raw[:].rearrange("p r (m t) -> p m t r", t=PACK)[:, :, 2 * g : 2 * g + 2, :])
            for g in range(2):
                cols = slice(g * HIDDEN // 2, (g + 1) * HIDDEN // 2)
                nc.vector.quantize_mx(out=w1_codes[:, cols].bitcast(FP8X4), scales=w1_bytes[:, cols],
                                      in_=w1_bf[g][:].rearrange("p c r -> p (c r)"))

        def first_product(t):
            bank = turns.tile([P, TARGETS], F32, name="mx_bank")
            cols = slice(t * P, (t + 1) * P)
            nc.tensor.matmul_mx(out=bank[:], lhsT=w1_codes[:, cols].bitcast(FP8X4), lhsT_scale=w1_bytes[:, cols],
                                rhs=x_codes[:].bitcast(FP8X4), rhs_scale=x_bytes[:], start=True, stop=True)
            tag = "dist_%d_%d" % (PACK - 1, t) if t < 2 else "y%d" % (t,)
            y.append(sb.tile([P, TARGETS], F32, name="y%d" % (t,), tag=tag, align_bytes=MX_ALIGN))
            nc.scalar.activation(y[t][:], bank[:], ACT.Copy, scale=unit_sb[:, t : t + 1])

        weights(0)
        nc.vector.tensor_copy(x_codes[:], x_word_table[:].bitcast(U32).indirect(offs_sb[:]))
        nc.vector.tensor_copy(x_bytes[:], x_scale_table[:].indirect(offs_sb[:]))
        weights(1)
        quantise_w1()
        weights(2)
        weights(3)
        for t in range(PACK):
            first_product(t)

        inv = [sb.tile([P, 2, HIDDEN], F32, name="inv0", tag="unit_sb"), sb.tile([P, 2, HIDDEN], F32, name="inv1")]
        sums = [sums_pool.tile([P, PACK, P], F32, name="sum%d" % (block,)) for block in range(TARGETS // P)]
        product_tags = ("cross_%d" % (PACK - 1,), "cov_%d" % (PACK - 1,), "products_last")

        def products(piece):
            j0, n = PIECES[piece]
            targets = slice(j0, j0 + n)
            entries = slice(j0 // PER_COLUMN, (j0 + n) // PER_COLUMN)
            prod = sb.tile([P, PACK, 2, n], F32, name="prod%d" % (piece,), tag=product_tags[piece])
            for group in row_groups(piece):
                t0, t1 = group[0], group[-1] + 1
                on_scalar = lists_on_scalar(piece, t0)
                if on_scalar:
                    picked = sb.tile([P, len(group), on_scalar, n], F32, name="picked%d_%d" % (piece, t0))
                    for l in range(on_scalar):
                        for t in group:
                            nc.scalar.activation(picked[:, t - t0, l, :], y[t][:].indirect(neighbours[l][:, entries]), ACT.Copy)
                for t in group:
                    for l in range(on_scalar, 2):
                        nc.vector.tensor_tensor(prod[:, t, l, :], y[t][:].indirect(neighbours[l][:, entries]),
                                                weight[:, t, l, targets], ALU.mult)
                if on_scalar:
                    nc.vector.tensor_tensor(prod[:, t0:t1, 0:on_scalar, :], picked[:],
                                            weight[:, t0:t1, 0:on_scalar, targets], ALU.mult)
                for t in group:
                    for b in range(n // P):
                        for l in range(2):
                            nc.tensor.matmul(sums[j0 // P + b][:, t, :], prod[:, t, l, b * P : (b + 1) * P], ident[:],
                                             is_transpose=True, start=(l == 0), stop=(l == 1))
            first = j0 // P
            nc.scalar.activation(inv[first // 2][:, first % 2 : first % 2 + n // P, :],
                                 dn_sq[:, first : first + n // P].rearrange("p b u q e -> p b (u q e)"), ACT.Abs_reciprocal_sqrt)

        sign = [sb.tile([P, HALF, PACK], BF16, name="sign0")]
        w2_bf = sb.tile([P, VARIABLES, PACK], BF16, name="w2_bf", align_bytes=MX_ALIGN)
        w2_codes = sb.tile([P, VARIABLES], U32, name="w2_codes", align_bytes=MX_ALIGN)
        w2_bytes = sb.tile([P, VARIABLES], U8, name="w2_bytes", align_bytes=MX_ALIGN)
        products(0)
        nc.vector.tensor_copy(*side_by_side(w2_bf[:], w2_raw[:]))
        nc.vector.tensor_scalar(*side_by_side(sign[0][:], rho_sq[:, :, 0:HALF]), PADDED_ONE / RHO_FACTOR, 0.5,
                                ALU.is_lt, ALU.subtract)
        nc.vector.quantize_mx(out=w2_codes[:].bitcast(FP8X4), scales=w2_bytes[:], in_=w2_bf[:].rearrange("p c r -> p (c r)"))
        products(1)
        products(LAST)

        sign.append(sb.tile([P, HALF, PACK], BF16, name="sign1", tag="y3", align_bytes=MX_ALIGN))
        nc.scalar.activation(*side_by_side(sign[1][:], rho_sq[:, :, HALF:TARGETS]), ACT.Sign, scale=-RHO_FACTOR, bias=PADDED_ONE)

        def finish(piece):
            j0, n = PIECES[piece]
            blocks = range(j0 // P, (j0 + n) // P)
            unsigned = sb.tile([P, len(blocks), HIDDEN], BF16, name="unsigned%d" % (piece,))
            bank = turns.tile([P, len(blocks), 2, P], F32, name="turn_bank")
            hid = sb.tile([P, n * PACK], BF16, name="hid%d" % (piece,), align_bytes=MX_ALIGN)
            for b, block in enumerate(blocks):
                nc.vector.tensor_tensor(unsigned[:, b, :].rearrange("p (u q e) -> p u q e", u=2, e=2),
                                        sums[block][:].rearrange("p (u e) q -> p u q e", e=2),
                                        inv[block // 2][:, block % 2, :].rearrange("p (u q e) -> p u q e", u=2, e=2), ALU.mult)
            for b in range(len(blocks)):
                words = unsigned[:, b, :].bitcast(F32)
                for u in range(2):
                    nc.tensor.transpose(bank[:, b, u, :], words[:, u * P : (u + 1) * P], ident[:])
            for b, block in enumerate(blocks):
                nc.vector.tensor_tensor(hid[:, b * HIDDEN : (b + 1) * HIDDEN].rearrange("p (j u e) -> p j u e", u=2, e=2),
                                        bank[:, b, :, :].bitcast(BF16).rearrange("p u (j e) -> p j u e", e=2),
                                        sign[block // 2][:, (block % 2) * P : (block % 2 + 1) * P, :].rearrange(
                                            "p j (u e) -> p j u e", e=2), ALU.mult)
            hid_codes = sb.tile([P, n], U32, name="hid_codes%d" % (piece,), align_bytes=MX_ALIGN)
            hid_bytes = sb.tile([P, n], U8, name="hid_bytes%d" % (piece,), align_bytes=MX_ALIGN)
            nc.vector.quantize_mx(out=hid_codes[:].bitcast(FP8X4), scales=hid_bytes[:], in_=hid[:])
            result_bank = turns.tile([P, n], F32, name="mx_bank")
            nc.tensor.matmul_mx(out=result_bank[:], lhsT=w2_codes[:].bitcast(FP8X4), lhsT_scale=w2_bytes[:],
                                rhs=hid_codes[:].bitcast(FP8X4), rhs_scale=hid_bytes[:], start=True, stop=True)
            result = sb.tile([P, n], F32, name="result%d" % (piece,))
            nc.scalar.copy(result[:], result_bank[:])
            nc.sync.dma_start(out[:, j0 : j0 + n], result[:])

        for piece in range(len(PIECES)):
            finish(piece)
